import numpy as np
import ml_dtypes

BF16 = ml_dtypes.bfloat16


def bf(x):
    return np.asarray(x, np.float32).astype(BF16)


def f32(x):
    return np.asarray(x, np.float32)


def f64(x):
    return np.asarray(x).astype(np.float64)


def striped(idx):
    return np.tile(idx.reshape(-1, 16).T, (8, 1))


S, K, M, N, E, Q = 2048, 128, 256, 4096, 8, 512


def two_experts():
    first = np.random.permutation(S).reshape(E, S // E)
    return np.concatenate([np.random.permutation(np.concatenate([first[e], first[(e + 1) % E]])) for e in range(E)])


def setup_inputs():
    return {"table": bf(np.random.standard_normal((K, S))), "w": bf(np.random.standard_normal((E, K, M)) / np.sqrt(K)), "c": f32(0.2 + 0.8 * np.random.random_sample((1, N))), "offs": striped(two_experts())}


def reference(table, w, c, offs):
    idx = offs[:16].T.reshape(-1)
    x = f64(table)[:, idx]
    y = np.concatenate([f64(w)[e].T @ x[:, e * Q : (e + 1) * Q] for e in range(E)], axis=1)
    return y * f64(c)

@@ -1,0 +1,42 @@
+import concourse.mybir as mybir
+
+EXPERTS, FEATURES, HIDDEN, TOKENS, PIECE = 8, 128, 256, 2048, 512
+ENTRIES = EXPERTS * PIECE
+P = 128
+HALVES = HIDDEN // P
+FLOPS = 2 * FEATURES * HIDDEN * ENTRIES
+
+BF16, F32, U16 = mybir.dt.bfloat16, mybir.dt.float32, mybir.dt.uint16
+
+
+def tile_gather_matmul_kernel(tc, table, w, c, offs, out):
+    nc = tc.nc
+    w_features_first = w.rearrange("e k m -> k e m")
+    with (
+        tc.tile_pool(name="held", bufs=1) as held,
+        tc.tile_pool(name="outs", bufs=EXPERTS * HALVES) as outs,
+        tc.psum_pool(name="banks", bufs=8) as banks,
+    ):
+        offsets = held.tile([P, ENTRIES // 16], U16, name="offsets")
+        tokens = held.tile([P, TOKENS], BF16, name="tokens")
+        weights = held.tile([P, EXPERTS, HIDDEN], BF16, name="weights")
+        factors = held.tile([P, ENTRIES], F32, name="factors")
+
+        nc.sync.dma_start(offsets[:], offs)
+        nc.scalar.dma_start(weights[:, 0, :], w_features_first[:, 0, :])
+        nc.sync.dma_start(tokens[:], table)
+        nc.scalar.dma_start(weights[:, 1:, :], w_features_first[:, 1:, :])
+        for e in range(EXPERTS):
+            piece = slice(e * PIECE, (e + 1) * PIECE)
+            nc.sync.dma_start(factors[:, piece], c[0, piece].partition_broadcast(P))
+
+        for e in range(EXPERTS):
+            piece = slice(e * PIECE, (e + 1) * PIECE)
+            picked = tokens[:].indirect(offsets[:, e * PIECE // 16 : (e + 1) * PIECE // 16])
+            for h in range(HALVES):
+                rows = slice(h * P, (h + 1) * P)
+                bank = banks.tile([P, PIECE], F32, name="bank")
+                nc.tensor.matmul(bank[:], weights[:, e, rows], picked, start=True, stop=True)
+                scaled = outs.tile([P, PIECE], F32, name="scaled")
+                nc.vector.tensor_tensor(scaled[:], bank[:], factors[:, piece], mybir.AluOpType.mult)
+                nc.scalar.dma_start(out[rows, piece], scaled[:])

@@ -1,17 +1,22 @@
 import concourse.mybir as mybir
+from concourse.masks import make_identity
 
 EXPERTS, FEATURES, HIDDEN, TOKENS, PIECE = 8, 128, 256, 2048, 512
 ENTRIES = EXPERTS * PIECE
 P = 128
 HALVES = HIDDEN // P
+QUAD = 32
+ROW = ENTRIES // QUAD
 FLOPS = 2 * FEATURES * HIDDEN * ENTRIES
 
 BF16, F32, U16 = mybir.dt.bfloat16, mybir.dt.float32, mybir.dt.uint16
+ADD, SUBTRACT, MULT = mybir.AluOpType.add, mybir.AluOpType.subtract, mybir.AluOpType.mult
 
 
 def tile_gather_matmul_kernel(tc, table, w, c, offs, out):
     nc = tc.nc
     w_features_first = w.rearrange("e k m -> k e m")
+    c_rows = c.rearrange("o (i q) -> (o i) q", q=ROW)
     with (
         tc.tile_pool(name="held", bufs=1) as held,
         tc.tile_pool(name="outs", bufs=EXPERTS * HALVES) as outs,
@@ -20,15 +25,42 @@ def tile_gather_matmul_kernel(tc, table, w, c, offs, out):
         offsets = held.tile([P, ENTRIES // 16], U16, name="offsets")
         tokens = held.tile([P, TOKENS], BF16, name="tokens")
         weights = held.tile([P, EXPERTS, HIDDEN], BF16, name="weights")
+        c_copies = held.tile([P, ROW], F32, name="c_copies")
+        c_rest = held.tile([P, ROW], F32, name="c_rest")
+        c_terms = held.tile([P, ROW], BF16, name="c_terms")
+        identity = held.tile([P, P], BF16, name="identity")
+        chooser = held.tile([P, QUAD], BF16, name="chooser")
         factors = held.tile([P, ENTRIES], F32, name="factors")
 
+        for g in range(P // QUAD):
+            queue = nc.sync if g % 2 == 0 else nc.scalar
+            queue.dma_start(c_copies[g * QUAD : (g + 1) * QUAD, :], c_rows)
         nc.sync.dma_start(offsets[:], offs)
         nc.scalar.dma_start(weights[:, 0, :], w_features_first[:, 0, :])
         nc.sync.dma_start(tokens[:], table)
         nc.scalar.dma_start(weights[:, 1:, :], w_features_first[:, 1:, :])
+
+        nc.vector.tensor_copy(c_terms[:], c_copies[:])
+        nc.vector.tensor_tensor(c_rest[64:, :], c_copies[64:, :], c_terms[64:, :], SUBTRACT)
+        nc.vector.tensor_copy(c_terms[64:, :], c_rest[64:, :])
+        nc.vector.tensor_tensor(c_terms[96:, :], c_rest[96:, :], c_terms[96:, :], SUBTRACT)
+
+        make_identity(nc, identity[:])
+        nc.vector.tensor_tensor(chooser[:], identity[:, 0:32], identity[:, 64:96], ADD)
+        nc.vector.tensor_tensor(chooser[:], chooser[:], identity[:, 96:128], ADD)
+
         for e in range(EXPERTS):
+            spread = banks.tile([P, PIECE], F32, name="bank")
+            for q in range(PIECE // ROW):
+                i = e * (PIECE // ROW) + q
+                nc.tensor.matmul(
+                    spread[:, q * ROW : (q + 1) * ROW], chooser[:, i : i + 1].to_broadcast([P, P]), c_terms[:], start=True, stop=True
+                )
             piece = slice(e * PIECE, (e + 1) * PIECE)
-            nc.sync.dma_start(factors[:, piece], c[0, piece].partition_broadcast(P))
+            if e % 2 == 0:
+                nc.scalar.copy(factors[:, piece], spread[:])
+            else:
+                nc.vector.tensor_copy(factors[:, piece], spread[:])
 
         for e in range(EXPERTS):
             piece = slice(e * PIECE, (e + 1) * PIECE)
@@ -38,5 +70,5 @@ def tile_gather_matmul_kernel(tc, table, w, c, offs, out):
                 bank = banks.tile([P, PIECE], F32, name="bank")
                 nc.tensor.matmul(bank[:], weights[:, e, rows], picked, start=True, stop=True)
                 scaled = outs.tile([P, PIECE], F32, name="scaled")
-                nc.vector.tensor_tensor(scaled[:], bank[:], factors[:, piece], mybir.AluOpType.mult)
-                nc.scalar.dma_start(out[rows, piece], scaled[:])
+                nc.vector.tensor_tensor(scaled[:], bank[:], factors[:, piece], MULT)
+                nc.sync.dma_start(out[rows, piece], scaled[:])

@@ -7,6 +7,8 @@ P = 128
 HALVES = HIDDEN // P
 QUAD = 32
 ROW = ENTRIES // QUAD
+EARLY = 2
+WARM_UP = 5
 FLOPS = 2 * FEATURES * HIDDEN * ENTRIES
 
 BF16, F32, U16 = mybir.dt.bfloat16, mybir.dt.float32, mybir.dt.uint16
@@ -26,43 +28,45 @@ def tile_gather_matmul_kernel(tc, table, w, c, offs, out):
         tokens = held.tile([P, TOKENS], BF16, name="tokens")
         weights = held.tile([P, EXPERTS, HIDDEN], BF16, name="weights")
         c_copies = held.tile([P, ROW], F32, name="c_copies")
-        c_rest = held.tile([P, ROW], F32, name="c_rest")
-        c_terms = held.tile([P, ROW], BF16, name="c_terms")
         identity = held.tile([P, P], BF16, name="identity")
         chooser = held.tile([P, QUAD], BF16, name="chooser")
         factors = held.tile([P, ENTRIES], F32, name="factors")
+        zeros = held.tile([P, PIECE], BF16, name="zeros")
+        early_copy = held.tile([P, 1], F32, name="early_copy")
 
         for g in range(P // QUAD):
             queue = nc.sync if g % 2 == 0 else nc.scalar
             queue.dma_start(c_copies[g * QUAD : (g + 1) * QUAD, :], c_rows)
         nc.sync.dma_start(offsets[:], offs)
-        nc.scalar.dma_start(weights[:, 0, :], w_features_first[:, 0, :])
+        nc.scalar.dma_start(weights[:, :EARLY, :], w_features_first[:, :EARLY, :])
         nc.sync.dma_start(tokens[:], table)
-        nc.scalar.dma_start(weights[:, 1:, :], w_features_first[:, 1:, :])
+        nc.sync.dma_start(weights[:, EARLY:, :], w_features_first[:, EARLY:, :])
 
-        nc.vector.tensor_copy(c_terms[:], c_copies[:])
-        nc.vector.tensor_tensor(c_rest[64:, :], c_copies[64:, :], c_terms[64:, :], SUBTRACT)
-        nc.vector.tensor_copy(c_terms[64:, :], c_rest[64:, :])
-        nc.vector.tensor_tensor(c_terms[96:, :], c_rest[96:, :], c_terms[96:, :], SUBTRACT)
+        nc.vector.memset(zeros[:], 0.0)
+        for turn in range(WARM_UP):
+            unread = banks.tile([P, PIECE], F32, name="bank")
+            nc.tensor.matmul(unread[:], zeros[:, 0:P], zeros[:], start=True, stop=True)
+
+        nc.scalar.copy(early_copy[:], zeros[:, 0:1])
+
+        upper = c_copies[:].bitcast(BF16).rearrange("p (q t) -> p q t", t=2)[:, :, 1]
+        nc.vector.tensor_tensor(c_copies[64:, :], c_copies[64:, :], upper[64:, :], SUBTRACT)
+        nc.vector.tensor_tensor(c_copies[96:, :], c_copies[96:, :], upper[96:, :], SUBTRACT)
 
         make_identity(nc, identity[:])
         nc.vector.tensor_tensor(chooser[:], identity[:, 0:32], identity[:, 64:96], ADD)
         nc.vector.tensor_tensor(chooser[:], chooser[:], identity[:, 96:128], ADD)
 
-        for e in range(EXPERTS):
+        def spread_factors(e):
             spread = banks.tile([P, PIECE], F32, name="bank")
             for q in range(PIECE // ROW):
                 i = e * (PIECE // ROW) + q
                 nc.tensor.matmul(
-                    spread[:, q * ROW : (q + 1) * ROW], chooser[:, i : i + 1].to_broadcast([P, P]), c_terms[:], start=True, stop=True
+                    spread[:, q * ROW : (q + 1) * ROW], chooser[:, i : i + 1].to_broadcast([P, P]), upper, start=True, stop=True
                 )
-            piece = slice(e * PIECE, (e + 1) * PIECE)
-            if e % 2 == 0:
-                nc.scalar.copy(factors[:, piece], spread[:])
-            else:
-                nc.vector.tensor_copy(factors[:, piece], spread[:])
+            nc.scalar.copy(factors[:, e * PIECE : (e + 1) * PIECE], spread[:])
 
-        for e in range(EXPERTS):
+        def multiply_scale_store(e):
             piece = slice(e * PIECE, (e + 1) * PIECE)
             picked = tokens[:].indirect(offsets[:, e * PIECE // 16 : (e + 1) * PIECE // 16])
             for h in range(HALVES):
@@ -72,3 +76,9 @@ def tile_gather_matmul_kernel(tc, table, w, c, offs, out):
                 scaled = outs.tile([P, PIECE], F32, name="scaled")
                 nc.vector.tensor_tensor(scaled[:], bank[:], factors[:, piece], MULT)
                 nc.sync.dma_start(out[rows, piece], scaled[:])
+
+        for group in (range(EARLY), range(EARLY, EXPERTS)):
+            for e in group:
+                spread_factors(e)
+            for e in group:
+                multiply_scale_store(e)

import concourse.mybir as mybir
from concourse.masks import make_identity

EXPERTS, FEATURES, HIDDEN, TOKENS, PIECE = 8, 128, 256, 2048, 512
ENTRIES = EXPERTS * PIECE
P = 128
HALVES = HIDDEN // P
QUAD = 32
ROW = ENTRIES // QUAD
EARLY = 2
WARM_UP = 5
FLOPS = 2 * FEATURES * HIDDEN * ENTRIES

BF16, F32, U16 = mybir.dt.bfloat16, mybir.dt.float32, mybir.dt.uint16
ADD, SUBTRACT, MULT = mybir.AluOpType.add, mybir.AluOpType.subtract, mybir.AluOpType.mult


def tile_gather_matmul_kernel(tc, table, w, c, offs, out):
    nc = tc.nc
    w_features_first = w.rearrange("e k m -> k e m")
    c_rows = c.rearrange("o (i q) -> (o i) q", q=ROW)
    with (
        tc.tile_pool(name="held", bufs=1) as held,
        tc.tile_pool(name="outs", bufs=EXPERTS * HALVES) as outs,
        tc.psum_pool(name="banks", bufs=8) as banks,
    ):
        offsets = held.tile([P, ENTRIES // 16], U16, name="offsets")
        tokens = held.tile([P, TOKENS], BF16, name="tokens")
        weights = held.tile([P, EXPERTS, HIDDEN], BF16, name="weights")
        c_copies = held.tile([P, ROW], F32, name="c_copies")
        identity = held.tile([P, P], BF16, name="identity")
        chooser = held.tile([P, QUAD], BF16, name="chooser")
        factors = held.tile([P, ENTRIES], F32, name="factors")
        zeros = held.tile([P, PIECE], BF16, name="zeros")
        early_copy = held.tile([P, 1], F32, name="early_copy")

        for g in range(P // QUAD):
            queue = nc.sync if g % 2 == 0 else nc.scalar
            queue.dma_start(c_copies[g * QUAD : (g + 1) * QUAD, :], c_rows)
        nc.sync.dma_start(offsets[:], offs)
        nc.scalar.dma_start(weights[:, :EARLY, :], w_features_first[:, :EARLY, :])
        nc.sync.dma_start(tokens[:], table)
        nc.sync.dma_start(weights[:, EARLY:, :], w_features_first[:, EARLY:, :])

        nc.vector.memset(zeros[:], 0.0)
        for turn in range(WARM_UP):
            unread = banks.tile([P, PIECE], F32, name="bank")
            nc.tensor.matmul(unread[:], zeros[:, 0:P], zeros[:], start=True, stop=True)

        nc.scalar.copy(early_copy[:], zeros[:, 0:1])

        upper = c_copies[:].bitcast(BF16).rearrange("p (q t) -> p q t", t=2)[:, :, 1]
        nc.vector.tensor_tensor(c_copies[64:, :], c_copies[64:, :], upper[64:, :], SUBTRACT)
        nc.vector.tensor_tensor(c_copies[96:, :], c_copies[96:, :], upper[96:, :], SUBTRACT)

        make_identity(nc, identity[:])
        nc.vector.tensor_tensor(chooser[:], identity[:, 0:32], identity[:, 64:96], ADD)
        nc.vector.tensor_tensor(chooser[:], chooser[:], identity[:, 96:128], ADD)

        def spread_factors(e):
            spread = banks.tile([P, PIECE], F32, name="bank")
            for q in range(PIECE // ROW):
                i = e * (PIECE // ROW) + q
                nc.tensor.matmul(
                    spread[:, q * ROW : (q + 1) * ROW], chooser[:, i : i + 1].to_broadcast([P, P]), upper, start=True, stop=True
                )
            nc.scalar.copy(factors[:, e * PIECE : (e + 1) * PIECE], spread[:])

        def multiply_scale_store(e):
            piece = slice(e * PIECE, (e + 1) * PIECE)
            picked = tokens[:].indirect(offsets[:, e * PIECE // 16 : (e + 1) * PIECE // 16])
            for h in range(HALVES):
                rows = slice(h * P, (h + 1) * P)
                bank = banks.tile([P, PIECE], F32, name="bank")
                nc.tensor.matmul(bank[:], weights[:, e, rows], picked, start=True, stop=True)
                scaled = outs.tile([P, PIECE], F32, name="scaled")
                nc.vector.tensor_tensor(scaled[:], bank[:], factors[:, piece], MULT)
                nc.sync.dma_start(out[rows, piece], scaled[:])

        for group in (range(EARLY), range(EARLY, EXPERTS)):
            for e in group:
                spread_factors(e)
            for e in group:
                multiply_scale_store(e)
